import numpy as np
import ml_dtypes


def mxq(x, axis, fmt="e4m3"):
    dtype, down = {"e4m3": (ml_dtypes.float8_e4m3fn, 7), "e5m2": (ml_dtypes.float8_e5m2, 14)}[fmt]
    v = np.moveaxis(np.asarray(x, np.float32).astype(ml_dtypes.bfloat16).astype(np.float64), axis, -1)
    blocks = v.reshape(v.shape[:-1] + (-1, 32))
    amax = np.abs(blocks).max(-1, keepdims=True)
    byte = np.maximum(np.where(amax > 0, np.frexp(amax)[1] - 1 + 127, 0) - down, 1)
    scale = np.exp2(byte - 127.0)
    codes = (blocks / scale).astype(np.float32).astype(dtype).astype(np.float64)
    return np.moveaxis((codes * scale).reshape(v.shape), -1, axis)


WIDE = False


def mx_kscale(k):
    if not WIDE:
        return np.ones(k)
    levels = np.array([10, -10, 5, -5, 0])
    if k % 512:
        return np.exp2(np.random.permutation(np.resize(levels, k // 32))).repeat(32)
    a = np.empty((k // 512, 16))
    for p in range(k // 512):
        a[p, :8] = np.random.permutation(np.resize(levels, 8))
        for g in range(8):
            far = levels[np.abs(levels - a[p, g]) >= 10]
            a[p, g + 8] = far[np.random.randint(len(far))]
    return np.exp2(a.ravel()).repeat(32)


def f64(x):
    return np.asarray(x).astype(np.float64)


def striped(idx):
    return np.tile(idx.reshape(-1, 16).T, (8, 1)).astype(np.uint16)


def unstriped(offs):
    return offs[:16].T.reshape(-1).astype(np.int64)


E2M1 = np.array([0.0, 0.5, 1.0, 1.5, 2.0, 3.0, 4.0, 6.0, -0.0, -0.5, -1.0, -1.5, -2.0, -3.0, -4.0, -6.0])


def pack_weight(w, fmt):
    k, n = w.shape
    w = f64(np.asarray(w, np.float32).astype(ml_dtypes.bfloat16)).reshape(k // 32, 32, n)
    amax = np.abs(w).max(1)
    if fmt == "e4m3":
        byte = np.frexp(amax)[1] - 1 + 127 - 7
    else:
        mant, ex = np.frexp(amax / 6.0)
        byte = np.where(mant > 0.5, ex, ex - 1) + 127
    byte = np.clip(np.where(amax > 0, byte, 1), 1, 254)
    scaled = (w * np.exp2(127.0 - byte)[:, None, :]).reshape(k, n).astype(np.float32)
    by_word = np.ascontiguousarray(scaled.reshape(k // 512, 128, 4, n).transpose(0, 1, 3, 2))
    if fmt == "e4m3":
        words = by_word.astype(ml_dtypes.float8_e4m3fn).view(np.uint8)
    else:
        c = by_word.astype(ml_dtypes.float4_e2m1fn).view(np.uint8) & 0xF
        words = (c[..., 0::2] | (c[..., 1::2] << 4)).reshape(k // 512, 128, 2 * n)
    return np.ascontiguousarray(words), np.ascontiguousarray(byte.astype(np.uint8).reshape(k // 512, 16, n))


def unpack_weight(words, scales, fmt):
    g, _, n = scales.shape
    words = np.ascontiguousarray(words).reshape(g, 128, n, -1)
    if fmt == "e4m3":
        vals = words.view(ml_dtypes.float8_e4m3fn).astype(np.float64)
    else:
        nib = np.empty((g, 128, n, 4), np.uint8)
        nib[..., 0::2] = words & 0xF
        nib[..., 1::2] = words >> 4
        vals = E2M1[nib]
    vals = vals * np.repeat(np.exp2(scales.astype(np.float64) - 127.0), 8, axis=1)[..., None]
    return vals.transpose(0, 1, 3, 2).reshape(g * 512, n)


def pack_table(v):
    words, scales = pack_weight(v, "e4m3")
    return np.concatenate([words.reshape(words.shape[0], -1), scales.reshape(scales.shape[0], -1)], axis=1)


def unpack_table(tab):
    g, t = tab.shape[0], tab.shape[1] // 528
    return unpack_weight(tab[:, :512 * t].reshape(g, 128, t, 4), tab[:, 512 * t:].reshape(g, 16, t), "e4m3")


K, R, M, T, S = 1536, 512, 1024, 1024, 256


def setup_inputs():
    n = np.random.standard_normal
    s = mx_kscale(K)[:, None]
    u = mx_kscale(R)[:, None]
    p_w4 = pack_weight(n((K, M)) / np.sqrt(K) / s, "e2m1")
    return {
        "tab": pack_table(n((K, T)) * s),
        "w4_words": p_w4[0],
        "w4_scales": p_w4[1],
        "down": (n((K, R)) / np.sqrt(K) / s * u.T).astype(np.float32),
        "up": (0.5 * n((R, M)) / np.sqrt(R) / u).astype(np.float32),
        "offs": striped(np.random.permutation(T)[:S]),
    }


def reference(tab, w4_words, w4_scales, down, up, offs):
    tab_ = unpack_table(tab)[:, unstriped(offs)]
    w4_ = unpack_weight(w4_words, w4_scales, "e2m1")
    down_ = mxq(f64(down), 0, "e4m3")
    up_ = mxq(f64(up), 0, "e4m3")
    h_ = mxq(down_.T @ tab_, 0, "e4m3")
    y = tab_.T @ w4_ + h_.T @ up_
    return y

@@ -1,0 +1,170 @@
+from contextlib import ExitStack
+
+import concourse.mybir as mybir
+
+K, R, M, T, S = 1536, 512, 1024, 1024, 256
+FLOPS = 2 * S * (K * R + K * M + R * M)
+
+F32 = mybir.dt.float32
+BF16 = mybir.dt.bfloat16
+I32 = mybir.dt.int32
+U32 = mybir.dt.uint32
+U16 = mybir.dt.uint16
+U8 = mybir.dt.uint8
+FP8X4 = mybir.dt.float8_e4m3fn_x4
+FP4X4 = mybir.dt.float4_e2m1fn_x4
+
+P = 128
+PASSES = K // 512
+N_TILE = 512
+WORD_COLS = 512 * T // 4
+
+
+def tile_list_tablora_tm_none_kernel(tc, tab, w4_words, w4_scales, down, up, offs, out):
+    nc = tc.nc
+    with ExitStack() as ctx:
+        keep = ctx.enter_context(tc.tile_pool(name="keep", bufs=1))
+        psum = ctx.enter_context(tc.psum_pool(name="psum", bufs=1))
+
+        offsets = keep.tile([P, S // 16], U16, name="offsets")
+        words = [keep.tile([P, T], I32, name=f"words{a}", align_bytes=64) for a in range(PASSES)]
+        tab_plane = keep.tile([P, PASSES * T // 4], I32, name="tab_plane", align_bytes=64)
+        w4_plane = keep.tile([P, PASSES * M // 4], I32, name="w4_plane", align_bytes=64)
+        w4 = keep.tile([P, PASSES, 2 * M], U8, name="w4", align_bytes=64)
+        d_raw = [keep.tile([P, 4, R], F32, name=f"d_raw{a}", align_bytes=64) for a in range(PASSES)]
+        d_grp = [keep.tile([P, 4, P, 4], BF16, name=f"d_grp{a}", align_bytes=64) for a in range(PASSES)]
+        d_codes = [keep.tile([P, R], U32, name=f"d_codes{a}", align_bytes=64) for a in range(PASSES)]
+        d_scales = [keep.tile([P, R], U8, name=f"d_scales{a}", align_bytes=64) for a in range(PASSES)]
+        u_raw = [keep.tile([P, 4, N_TILE], F32, name=f"u_raw{n}", align_bytes=64) for n in range(2)]
+        u_grp = [keep.tile([P, N_TILE, 4], BF16, name=f"u_grp{n}", align_bytes=64) for n in range(2)]
+        u_codes = [keep.tile([P, N_TILE], U32, name=f"u_codes{n}", align_bytes=64) for n in range(2)]
+        u_scales = [keep.tile([P, N_TILE], U8, name=f"u_scales{n}", align_bytes=64) for n in range(2)]
+        v_codes = [keep.tile([P, S], U32, name=f"v_codes{a}", align_bytes=64) for a in range(PASSES)]
+        v_scales = [keep.tile([P, S], U8, name=f"v_scales{a}", align_bytes=64) for a in range(PASSES)]
+        h_grp = [keep.tile([P, P, 4], BF16, name=f"h_grp{j}", align_bytes=64) for j in range(2)]
+        h_codes = [keep.tile([P, P], U32, name=f"h_codes{j}", align_bytes=64) for j in range(2)]
+        h_scales = [keep.tile([P, P], U8, name=f"h_scales{j}", align_bytes=64) for j in range(2)]
+        o_sb = [[keep.tile([P, N_TILE], F32, name=f"o_sb{j}{n}", align_bytes=64) for n in range(2)] for j in range(2)]
+        h_ps = [psum.tile([P, 4, P], F32, name=f"h_ps{j}") for j in range(2)]
+        o_ps = [[psum.tile([P, N_TILE], F32, name=f"o_ps{j}{n}") for n in range(2)] for j in range(2)]
+
+        nc.vector.memset(tab_plane[:], 0)
+        nc.vector.memset(w4_plane[:], 0)
+        nc.sync.dma_start(offsets[:], offs)
+        tab_i = tab.bitcast(I32)
+        tab_s = tab_i[:, WORD_COLS:].rearrange("a (q r t) -> r q a t", q=4, r=4)
+        w4_s = w4_scales.bitcast(I32).rearrange("a (q r) n -> r q a n", q=4, r=4)
+        def load_pass(a):
+            nc.sync.dma_start(out=words[a][:], in_=tab_i[a, :WORD_COLS].rearrange("(p t) -> p t", p=P))
+            nc.sync.dma_start(
+                out=d_raw[a][:], in_=down[512 * a : 512 * (a + 1), :].rearrange("(p j) r -> p j r", j=4)
+            )
+
+        def load_scales(plane, rows):
+            for r in range(4):
+                nc.sync.dma_start(out=plane[r:P:32, :].rearrange("q (a t) -> q a t", a=PASSES), in_=rows[r])
+
+        load_pass(0)
+        load_scales(tab_plane, tab_s)
+        load_pass(1)
+        load_pass(2)
+        load_scales(w4_plane, w4_s)
+        up_v = up.rearrange("(p j) n -> p j n", j=4)
+        nc.sync.dma_start(out=u_raw[0][:], in_=up_v[:, :, 0:N_TILE])
+        nc.sync.dma_start(out=w4[:].bitcast(I32), in_=w4_words.bitcast(I32).rearrange("a p n -> p a n"))
+        nc.sync.dma_start(out=u_raw[1][:], in_=up_v[:, :, N_TILE:])
+
+        tab_bytes = tab_plane[:].bitcast(U8)
+        w4_bytes = w4_plane[:].bitcast(U8)
+
+        for a in range(PASSES):
+            nc.vector.tensor_copy(v_codes[a][:], words[a][:].bitcast(U32).indirect(offsets[:]))
+            nc.vector.tensor_copy(v_scales[a][:], tab_bytes[:, a * T : (a + 1) * T].indirect(offsets[:]))
+            src = d_raw[a][:].rearrange("p j (m t) -> p m j t", t=4)
+            dst = d_grp[a][:].rearrange("p t m j -> p m j t")
+            nc.vector.tensor_copy(out=dst[:, :, :, 0:2], in_=src[:, :, :, 0:2])
+            nc.scalar.copy(out=dst[:, :, :, 2:4], in_=src[:, :, :, 2:4])
+            for c in range(2):
+                cols = slice(256 * c, 256 * (c + 1))
+                nc.vector.quantize_mx(
+                    out=d_codes[a][:, cols].bitcast(FP8X4),
+                    scales=d_scales[a][:, cols],
+                    in_=d_grp[a][:, 2 * c : 2 * c + 2].rearrange("p t m j -> p (t m j)"),
+                )
+
+        def prepare_up(n):
+            src = u_raw[n][:].rearrange("p j (c i) -> p c j i", i=4)
+            dst = u_grp[n][:].rearrange("p (c i) j -> p c j i", i=4)
+            nc.vector.tensor_copy(out=dst[:, 0:64], in_=src[:, 0:64])
+            nc.scalar.copy(out=dst[:, 64:128], in_=src[:, 64:128])
+            for c in range(2):
+                cols = slice(256 * c, 256 * (c + 1))
+                nc.vector.quantize_mx(
+                    out=u_codes[n][:, cols].bitcast(FP8X4),
+                    scales=u_scales[n][:, cols],
+                    in_=u_grp[n][:, cols, :].rearrange("p w j -> p (w j)"),
+                )
+
+        prepare_up(0)
+
+        for j in range(2):
+            js = slice(P * j, P * (j + 1))
+            for t in range(4):
+                ts = slice(P * t, P * (t + 1))
+                for a in range(PASSES):
+                    nc.tensor.matmul_mx(
+                        out=h_ps[j][:, t, :],
+                        lhsT=d_codes[a][:, ts].bitcast(FP8X4),
+                        lhsT_scale=d_scales[a][:, ts],
+                        rhs=v_codes[a][:, js].bitcast(FP8X4),
+                        rhs_scale=v_scales[a][:, js],
+                        start=(a == 0),
+                        stop=(a == PASSES - 1),
+                    )
+            hv = h_ps[j][:].rearrange("p t j -> p j t")
+            if j == 0:
+                nc.vector.tensor_copy(out=h_grp[j][:], in_=hv)
+            else:
+                nc.scalar.copy(out=h_grp[j][:], in_=hv)
+            nc.vector.quantize_mx(
+                out=h_codes[j][:].bitcast(FP8X4),
+                scales=h_scales[j][:],
+                in_=h_grp[j][:].rearrange("p w j -> p (w j)"),
+            )
+
+        for a in range(PASSES):
+            for n in range(2):
+                for j in range(2):
+                    js = slice(P * j, P * (j + 1))
+                    nc.tensor.matmul_mx(
+                        out=o_ps[j][n][:],
+                        lhsT=v_codes[a][:, js].bitcast(FP8X4),
+                        lhsT_scale=v_scales[a][:, js],
+                        rhs=w4[:, a, 1024 * n : 1024 * (n + 1)].bitcast(FP4X4),
+                        rhs_scale=w4_bytes[:, a * M + N_TILE * n : a * M + N_TILE * (n + 1)],
+                        start=(a == 0),
+                        stop=False,
+                    )
+
+        def finish(n):
+            for j in range(2):
+                nc.tensor.matmul_mx(
+                    out=o_ps[j][n][:],
+                    lhsT=h_codes[j][:].bitcast(FP8X4),
+                    lhsT_scale=h_scales[j][:],
+                    rhs=u_codes[n][:].bitcast(FP8X4),
+                    rhs_scale=u_scales[n][:],
+                    start=False,
+                    stop=True,
+                )
+                if j == 0:
+                    nc.vector.tensor_copy(out=o_sb[j][n][:], in_=o_ps[j][n][:])
+                else:
+                    nc.scalar.copy(out=o_sb[j][n][:], in_=o_ps[j][n][:])
+                nc.sync.dma_start(
+                    out=out[P * j : P * (j + 1), N_TILE * n : N_TILE * (n + 1)], in_=o_sb[j][n][:]
+                )
+
+        finish(0)
+        prepare_up(1)
+        finish(1)

@@ -17,6 +17,10 @@ FP4X4 = mybir.dt.float4_e2m1fn_x4
 P = 128
 PASSES = K // 512
 N_TILE = 512
+U_STARTS = (0, 256, 512, 768)
+U_WIDTHS = (256, 256, 256, 256)
+U_VECTOR = (256, 0, 0, 256)
+CHUNKS = len(U_STARTS)
 WORD_COLS = 512 * T // 4
 
 
@@ -35,17 +39,18 @@ def tile_list_tablora_tm_none_kernel(tc, tab, w4_words, w4_scales, down, up, off
         d_grp = [keep.tile([P, 4, P, 4], BF16, name=f"d_grp{a}", align_bytes=64) for a in range(PASSES)]
         d_codes = [keep.tile([P, R], U32, name=f"d_codes{a}", align_bytes=64) for a in range(PASSES)]
         d_scales = [keep.tile([P, R], U8, name=f"d_scales{a}", align_bytes=64) for a in range(PASSES)]
-        u_raw = [keep.tile([P, 4, N_TILE], F32, name=f"u_raw{n}", align_bytes=64) for n in range(2)]
+        u_raw = [keep.tile([P, 4, U_WIDTHS[c]], F32, name=f"u_raw{c}", align_bytes=64) for c in range(CHUNKS)]
         u_grp = [keep.tile([P, N_TILE, 4], BF16, name=f"u_grp{n}", align_bytes=64) for n in range(2)]
         u_codes = [keep.tile([P, N_TILE], U32, name=f"u_codes{n}", align_bytes=64) for n in range(2)]
         u_scales = [keep.tile([P, N_TILE], U8, name=f"u_scales{n}", align_bytes=64) for n in range(2)]
         v_codes = [keep.tile([P, S], U32, name=f"v_codes{a}", align_bytes=64) for a in range(PASSES)]
         v_scales = [keep.tile([P, S], U8, name=f"v_scales{a}", align_bytes=64) for a in range(PASSES)]
-        h_grp = [keep.tile([P, P, 4], BF16, name=f"h_grp{j}", align_bytes=64) for j in range(2)]
-        h_codes = [keep.tile([P, P], U32, name=f"h_codes{j}", align_bytes=64) for j in range(2)]
-        h_scales = [keep.tile([P, P], U8, name=f"h_scales{j}", align_bytes=64) for j in range(2)]
+        h_raw = keep.tile([P, 4, S], BF16, name="h_raw", align_bytes=64)
+        h_grp = keep.tile([P, S, 4], BF16, name="h_grp", align_bytes=64)
+        h_codes = keep.tile([P, S], U32, name="h_codes", align_bytes=64)
+        h_scales = keep.tile([P, S], U8, name="h_scales", align_bytes=64)
         o_sb = [[keep.tile([P, N_TILE], F32, name=f"o_sb{j}{n}", align_bytes=64) for n in range(2)] for j in range(2)]
-        h_ps = [psum.tile([P, 4, P], F32, name=f"h_ps{j}") for j in range(2)]
+        h_ps = [psum.tile([P, S], F32, name=f"h_ps{t}") for t in range(4)]
         o_ps = [[psum.tile([P, N_TILE], F32, name=f"o_ps{j}{n}") for n in range(2)] for j in range(2)]
 
         nc.vector.memset(tab_plane[:], 0)
@@ -54,8 +59,10 @@ def tile_list_tablora_tm_none_kernel(tc, tab, w4_words, w4_scales, down, up, off
         tab_i = tab.bitcast(I32)
         tab_s = tab_i[:, WORD_COLS:].rearrange("a (q r t) -> r q a t", q=4, r=4)
         w4_s = w4_scales.bitcast(I32).rearrange("a (q r) n -> r q a n", q=4, r=4)
-        def load_pass(a):
+        def load_words(a):
             nc.sync.dma_start(out=words[a][:], in_=tab_i[a, :WORD_COLS].rearrange("(p t) -> p t", p=P))
+
+        def load_down(a):
             nc.sync.dma_start(
                 out=d_raw[a][:], in_=down[512 * a : 512 * (a + 1), :].rearrange("(p j) r -> p j r", j=4)
             )
@@ -64,107 +71,148 @@ def tile_list_tablora_tm_none_kernel(tc, tab, w4_words, w4_scales, down, up, off
             for r in range(4):
                 nc.sync.dma_start(out=plane[r:P:32, :].rearrange("q (a t) -> q a t", a=PASSES), in_=rows[r])
 
-        load_pass(0)
+        load_down(0)
         load_scales(tab_plane, tab_s)
-        load_pass(1)
-        load_pass(2)
+        load_down(1)
+        load_words(0)
+        load_words(1)
+        load_down(2)
         load_scales(w4_plane, w4_s)
-        up_v = up.rearrange("(p j) n -> p j n", j=4)
-        nc.sync.dma_start(out=u_raw[0][:], in_=up_v[:, :, 0:N_TILE])
         nc.sync.dma_start(out=w4[:].bitcast(I32), in_=w4_words.bitcast(I32).rearrange("a p n -> p a n"))
-        nc.sync.dma_start(out=u_raw[1][:], in_=up_v[:, :, N_TILE:])
+        load_words(2)
+        up_v = up.rearrange("(p j) n -> p j n", j=4)
+        for c in range(CHUNKS):
+            nc.sync.dma_start(out=u_raw[c][:], in_=up_v[:, :, U_STARTS[c] : U_STARTS[c] + U_WIDTHS[c]])
 
         tab_bytes = tab_plane[:].bitcast(U8)
         w4_bytes = w4_plane[:].bitcast(U8)
 
-        for a in range(PASSES):
+        def gather_words(a):
             nc.vector.tensor_copy(v_codes[a][:], words[a][:].bitcast(U32).indirect(offsets[:]))
+
+        def gather_scales(a):
             nc.vector.tensor_copy(v_scales[a][:], tab_bytes[:, a * T : (a + 1) * T].indirect(offsets[:]))
+
+        def group_down(a):
             src = d_raw[a][:].rearrange("p j (m t) -> p m j t", t=4)
             dst = d_grp[a][:].rearrange("p t m j -> p m j t")
-            nc.vector.tensor_copy(out=dst[:, :, :, 0:2], in_=src[:, :, :, 0:2])
-            nc.scalar.copy(out=dst[:, :, :, 2:4], in_=src[:, :, :, 2:4])
-            for c in range(2):
-                cols = slice(256 * c, 256 * (c + 1))
-                nc.vector.quantize_mx(
-                    out=d_codes[a][:, cols].bitcast(FP8X4),
-                    scales=d_scales[a][:, cols],
-                    in_=d_grp[a][:, 2 * c : 2 * c + 2].rearrange("p t m j -> p (t m j)"),
-                )
-
-        def prepare_up(n):
-            src = u_raw[n][:].rearrange("p j (c i) -> p c j i", i=4)
-            dst = u_grp[n][:].rearrange("p (c i) j -> p c j i", i=4)
-            nc.vector.tensor_copy(out=dst[:, 0:64], in_=src[:, 0:64])
-            nc.scalar.copy(out=dst[:, 64:128], in_=src[:, 64:128])
-            for c in range(2):
-                cols = slice(256 * c, 256 * (c + 1))
-                nc.vector.quantize_mx(
-                    out=u_codes[n][:, cols].bitcast(FP8X4),
-                    scales=u_scales[n][:, cols],
-                    in_=u_grp[n][:, cols, :].rearrange("p w j -> p (w j)"),
-                )
-
-        prepare_up(0)
-
-        for j in range(2):
-            js = slice(P * j, P * (j + 1))
-            for t in range(4):
-                ts = slice(P * t, P * (t + 1))
-                for a in range(PASSES):
-                    nc.tensor.matmul_mx(
-                        out=h_ps[j][:, t, :],
-                        lhsT=d_codes[a][:, ts].bitcast(FP8X4),
-                        lhsT_scale=d_scales[a][:, ts],
-                        rhs=v_codes[a][:, js].bitcast(FP8X4),
-                        rhs_scale=v_scales[a][:, js],
-                        start=(a == 0),
-                        stop=(a == PASSES - 1),
-                    )
-            hv = h_ps[j][:].rearrange("p t j -> p j t")
-            if j == 0:
-                nc.vector.tensor_copy(out=h_grp[j][:], in_=hv)
+            if a < 2:
+                nc.scalar.copy(out=dst, in_=src)
             else:
-                nc.scalar.copy(out=h_grp[j][:], in_=hv)
+                nc.vector.tensor_copy(out=dst, in_=src)
+
+        def quantize_down(a):
             nc.vector.quantize_mx(
-                out=h_codes[j][:].bitcast(FP8X4),
-                scales=h_scales[j][:],
-                in_=h_grp[j][:].rearrange("p w j -> p (w j)"),
+                out=d_codes[a][:].bitcast(FP8X4),
+                scales=d_scales[a][:],
+                in_=d_grp[a][:].rearrange("p t m j -> p (t m j)"),
             )
 
-        for a in range(PASSES):
-            for n in range(2):
-                for j in range(2):
-                    js = slice(P * j, P * (j + 1))
-                    nc.tensor.matmul_mx(
-                        out=o_ps[j][n][:],
-                        lhsT=v_codes[a][:, js].bitcast(FP8X4),
-                        lhsT_scale=v_scales[a][:, js],
-                        rhs=w4[:, a, 1024 * n : 1024 * (n + 1)].bitcast(FP4X4),
-                        rhs_scale=w4_bytes[:, a * M + N_TILE * n : a * M + N_TILE * (n + 1)],
-                        start=(a == 0),
-                        stop=False,
-                    )
+        def prepare_up(c):
+            n, first, width, v = U_STARTS[c] // N_TILE, U_STARTS[c] % N_TILE, U_WIDTHS[c], U_VECTOR[c]
+            src = u_raw[c][:].rearrange("p j (c i) -> p c j i", i=4)
+            dst = u_grp[n][:, first : first + width, :].rearrange("p (c i) j -> p c j i", i=4)
+            if v > 0:
+                nc.vector.tensor_copy(out=dst[:, 0 : v // 4], in_=src[:, 0 : v // 4])
+            if v < width:
+                nc.scalar.copy(out=dst[:, v // 4 : width // 4], in_=src[:, v // 4 : width // 4])
+            cols = slice(first, first + width)
+            nc.vector.quantize_mx(
+                out=u_codes[n][:, cols].bitcast(FP8X4),
+                scales=u_scales[n][:, cols],
+                in_=u_grp[n][:, cols, :].rearrange("p w j -> p (w j)"),
+            )
 
-        def finish(n):
+        def base(a, n):
             for j in range(2):
+                js = slice(P * j, P * (j + 1))
                 nc.tensor.matmul_mx(
                     out=o_ps[j][n][:],
-                    lhsT=h_codes[j][:].bitcast(FP8X4),
-                    lhsT_scale=h_scales[j][:],
-                    rhs=u_codes[n][:].bitcast(FP8X4),
-                    rhs_scale=u_scales[n][:],
-                    start=False,
-                    stop=True,
+                    lhsT=v_codes[a][:, js].bitcast(FP8X4),
+                    lhsT_scale=v_scales[a][:, js],
+                    rhs=w4[:, a, 1024 * n : 1024 * (n + 1)].bitcast(FP4X4),
+                    rhs_scale=w4_bytes[:, a * M + N_TILE * n : a * M + N_TILE * (n + 1)],
+                    start=(a == 0),
+                    stop=False,
                 )
+
+        def low_rank(a):
+            for t in range(4):
+                ts = slice(P * t, P * (t + 1))
+                nc.tensor.matmul_mx(
+                    out=h_ps[t][:],
+                    lhsT=d_codes[a][:, ts].bitcast(FP8X4),
+                    lhsT_scale=d_scales[a][:, ts],
+                    rhs=v_codes[a][:].bitcast(FP8X4),
+                    rhs_scale=v_scales[a][:],
+                    start=(a == 0),
+                    stop=(a == PASSES - 1),
+                )
+
+        def close(c):
+            n, first, width = U_STARTS[c] // N_TILE, U_STARTS[c] % N_TILE, U_WIDTHS[c]
+            cols = slice(first, first + width)
+            for j in range(2):
+                nc.tensor.matmul_mx(
+                    out=o_ps[j][n][:, cols],
+                    lhsT=h_codes[:, P * j : P * (j + 1)].bitcast(FP8X4),
+                    lhsT_scale=h_scales[:, P * j : P * (j + 1)],
+                    rhs=u_codes[n][:, cols].bitcast(FP8X4),
+                    rhs_scale=u_scales[n][:, cols],
+                    start=False,
+                    stop=(first + width == N_TILE),
+                )
+
+        def store(n):
+            for j in range(2):
                 if j == 0:
                     nc.vector.tensor_copy(out=o_sb[j][n][:], in_=o_ps[j][n][:])
                 else:
                     nc.scalar.copy(out=o_sb[j][n][:], in_=o_ps[j][n][:])
-                nc.sync.dma_start(
+                queue = nc.sync if j == 0 else nc.scalar
+                queue.dma_start(
                     out=out[P * j : P * (j + 1), N_TILE * n : N_TILE * (n + 1)], in_=o_sb[j][n][:]
                 )
 
-        finish(0)
+        group_down(0)
+        for a in range(PASSES):
+            gather_scales(a)
+        group_down(1)
+        quantize_down(0)
+        gather_words(0)
+        low_rank(0)
+        quantize_down(1)
+        gather_words(1)
+        low_rank(1)
+        group_down(2)
+        quantize_down(2)
+        base(0, 0)
+        base(0, 1)
+        gather_words(2)
+        low_rank(2)
+        for t in range(4):
+            if t < 2:
+                nc.vector.tensor_copy(out=h_raw[:, t, :], in_=h_ps[t][:])
+            else:
+                nc.scalar.copy(out=h_raw[:, t, :], in_=h_ps[t][:])
+        nc.vector.tensor_copy(
+            out=h_grp[:].rearrange("p (c i) t -> p c t i", i=8),
+            in_=h_raw[:].rearrange("p t (c i) -> p c t i", i=8),
+        )
+        nc.vector.quantize_mx(
+            out=h_codes[:].bitcast(FP8X4), scales=h_scales[:], in_=h_grp[:].rearrange("p w j -> p (w j)")
+        )
+        base(1, 0)
+        base(2, 0)
+        prepare_up(0)
         prepare_up(1)
-        finish(1)
+        close(0)
+        close(1)
+        base(1, 1)
+        base(2, 1)
+        prepare_up(2)
+        store(0)
+        close(2)
+        prepare_up(3)
+        close(3)
+        store(1)

@@ -163,15 +163,16 @@ def tile_list_tablora_tm_none_kernel(tc, tab, w4_words, w4_scales, down, up, off
                     stop=(first + width == N_TILE),
                 )
 
-        def store(n):
+        def store(n, first, width):
+            cols = slice(first, first + width)
             for j in range(2):
-                if j == 0:
-                    nc.vector.tensor_copy(out=o_sb[j][n][:], in_=o_ps[j][n][:])
+                if j == 0 and n == 1:
+                    nc.vector.tensor_copy(out=o_sb[j][n][:, cols], in_=o_ps[j][n][:, cols])
                 else:
-                    nc.scalar.copy(out=o_sb[j][n][:], in_=o_ps[j][n][:])
-                queue = nc.sync if j == 0 else nc.scalar
-                queue.dma_start(
-                    out=out[P * j : P * (j + 1), N_TILE * n : N_TILE * (n + 1)], in_=o_sb[j][n][:]
+                    nc.scalar.copy(out=o_sb[j][n][:, cols], in_=o_ps[j][n][:, cols])
+                nc.sync.dma_start(
+                    out=out[P * j : P * (j + 1), N_TILE * n + first : N_TILE * n + first + width],
+                    in_=o_sb[j][n][:, cols],
                 )
 
         group_down(0)
@@ -186,10 +187,13 @@ def tile_list_tablora_tm_none_kernel(tc, tab, w4_words, w4_scales, down, up, off
         low_rank(1)
         group_down(2)
         quantize_down(2)
-        base(0, 0)
-        base(0, 1)
+        for a in range(2):
+            for n in range(2):
+                base(a, n)
         gather_words(2)
         low_rank(2)
+        base(2, 0)
+        base(2, 1)
         for t in range(4):
             if t < 2:
                 nc.vector.tensor_copy(out=h_raw[:, t, :], in_=h_ps[t][:])
@@ -202,17 +206,14 @@ def tile_list_tablora_tm_none_kernel(tc, tab, w4_words, w4_scales, down, up, off
         nc.vector.quantize_mx(
             out=h_codes[:].bitcast(FP8X4), scales=h_scales[:], in_=h_grp[:].rearrange("p w j -> p (w j)")
         )
-        base(1, 0)
-        base(2, 0)
         prepare_up(0)
         prepare_up(1)
         close(0)
         close(1)
-        base(1, 1)
-        base(2, 1)
         prepare_up(2)
-        store(0)
+        store(0, 0, N_TILE)
         close(2)
         prepare_up(3)
         close(3)
-        store(1)
+        store(1, 0, N_TILE // 2)
+        store(1, N_TILE // 2, N_TILE // 2)

from contextlib import ExitStack

import concourse.mybir as mybir

K, R, M, T, S = 1536, 512, 1024, 1024, 256
FLOPS = 2 * S * (K * R + K * M + R * M)

F32 = mybir.dt.float32
BF16 = mybir.dt.bfloat16
I32 = mybir.dt.int32
U32 = mybir.dt.uint32
U16 = mybir.dt.uint16
U8 = mybir.dt.uint8
FP8X4 = mybir.dt.float8_e4m3fn_x4
FP4X4 = mybir.dt.float4_e2m1fn_x4

P = 128
PASSES = K // 512
N_TILE = 512
U_STARTS = (0, 256, 512, 768)
U_WIDTHS = (256, 256, 256, 256)
U_VECTOR = (256, 0, 0, 256)
CHUNKS = len(U_STARTS)
WORD_COLS = 512 * T // 4


def tile_list_tablora_tm_none_kernel(tc, tab, w4_words, w4_scales, down, up, offs, out):
    nc = tc.nc
    with ExitStack() as ctx:
        keep = ctx.enter_context(tc.tile_pool(name="keep", bufs=1))
        psum = ctx.enter_context(tc.psum_pool(name="psum", bufs=1))

        offsets = keep.tile([P, S // 16], U16, name="offsets")
        words = [keep.tile([P, T], I32, name=f"words{a}", align_bytes=64) for a in range(PASSES)]
        tab_plane = keep.tile([P, PASSES * T // 4], I32, name="tab_plane", align_bytes=64)
        w4_plane = keep.tile([P, PASSES * M // 4], I32, name="w4_plane", align_bytes=64)
        w4 = keep.tile([P, PASSES, 2 * M], U8, name="w4", align_bytes=64)
        d_raw = [keep.tile([P, 4, R], F32, name=f"d_raw{a}", align_bytes=64) for a in range(PASSES)]
        d_grp = [keep.tile([P, 4, P, 4], BF16, name=f"d_grp{a}", align_bytes=64) for a in range(PASSES)]
        d_codes = [keep.tile([P, R], U32, name=f"d_codes{a}", align_bytes=64) for a in range(PASSES)]
        d_scales = [keep.tile([P, R], U8, name=f"d_scales{a}", align_bytes=64) for a in range(PASSES)]
        u_raw = [keep.tile([P, 4, U_WIDTHS[c]], F32, name=f"u_raw{c}", align_bytes=64) for c in range(CHUNKS)]
        u_grp = [keep.tile([P, N_TILE, 4], BF16, name=f"u_grp{n}", align_bytes=64) for n in range(2)]
        u_codes = [keep.tile([P, N_TILE], U32, name=f"u_codes{n}", align_bytes=64) for n in range(2)]
        u_scales = [keep.tile([P, N_TILE], U8, name=f"u_scales{n}", align_bytes=64) for n in range(2)]
        v_codes = [keep.tile([P, S], U32, name=f"v_codes{a}", align_bytes=64) for a in range(PASSES)]
        v_scales = [keep.tile([P, S], U8, name=f"v_scales{a}", align_bytes=64) for a in range(PASSES)]
        h_raw = keep.tile([P, 4, S], BF16, name="h_raw", align_bytes=64)
        h_grp = keep.tile([P, S, 4], BF16, name="h_grp", align_bytes=64)
        h_codes = keep.tile([P, S], U32, name="h_codes", align_bytes=64)
        h_scales = keep.tile([P, S], U8, name="h_scales", align_bytes=64)
        o_sb = [[keep.tile([P, N_TILE], F32, name=f"o_sb{j}{n}", align_bytes=64) for n in range(2)] for j in range(2)]
        h_ps = [psum.tile([P, S], F32, name=f"h_ps{t}") for t in range(4)]
        o_ps = [[psum.tile([P, N_TILE], F32, name=f"o_ps{j}{n}") for n in range(2)] for j in range(2)]

        nc.vector.memset(tab_plane[:], 0)
        nc.vector.memset(w4_plane[:], 0)
        nc.sync.dma_start(offsets[:], offs)
        tab_i = tab.bitcast(I32)
        tab_s = tab_i[:, WORD_COLS:].rearrange("a (q r t) -> r q a t", q=4, r=4)
        w4_s = w4_scales.bitcast(I32).rearrange("a (q r) n -> r q a n", q=4, r=4)
        def load_words(a):
            nc.sync.dma_start(out=words[a][:], in_=tab_i[a, :WORD_COLS].rearrange("(p t) -> p t", p=P))

        def load_down(a):
            nc.sync.dma_start(
                out=d_raw[a][:], in_=down[512 * a : 512 * (a + 1), :].rearrange("(p j) r -> p j r", j=4)
            )

        def load_scales(plane, rows):
            for r in range(4):
                nc.sync.dma_start(out=plane[r:P:32, :].rearrange("q (a t) -> q a t", a=PASSES), in_=rows[r])

        load_down(0)
        load_scales(tab_plane, tab_s)
        load_down(1)
        load_words(0)
        load_words(1)
        load_down(2)
        load_scales(w4_plane, w4_s)
        nc.sync.dma_start(out=w4[:].bitcast(I32), in_=w4_words.bitcast(I32).rearrange("a p n -> p a n"))
        load_words(2)
        up_v = up.rearrange("(p j) n -> p j n", j=4)
        for c in range(CHUNKS):
            nc.sync.dma_start(out=u_raw[c][:], in_=up_v[:, :, U_STARTS[c] : U_STARTS[c] + U_WIDTHS[c]])

        tab_bytes = tab_plane[:].bitcast(U8)
        w4_bytes = w4_plane[:].bitcast(U8)

        def gather_words(a):
            nc.vector.tensor_copy(v_codes[a][:], words[a][:].bitcast(U32).indirect(offsets[:]))

        def gather_scales(a):
            nc.vector.tensor_copy(v_scales[a][:], tab_bytes[:, a * T : (a + 1) * T].indirect(offsets[:]))

        def group_down(a):
            src = d_raw[a][:].rearrange("p j (m t) -> p m j t", t=4)
            dst = d_grp[a][:].rearrange("p t m j -> p m j t")
            if a < 2:
                nc.scalar.copy(out=dst, in_=src)
            else:
                nc.vector.tensor_copy(out=dst, in_=src)

        def quantize_down(a):
            nc.vector.quantize_mx(
                out=d_codes[a][:].bitcast(FP8X4),
                scales=d_scales[a][:],
                in_=d_grp[a][:].rearrange("p t m j -> p (t m j)"),
            )

        def prepare_up(c):
            n, first, width, v = U_STARTS[c] // N_TILE, U_STARTS[c] % N_TILE, U_WIDTHS[c], U_VECTOR[c]
            src = u_raw[c][:].rearrange("p j (c i) -> p c j i", i=4)
            dst = u_grp[n][:, first : first + width, :].rearrange("p (c i) j -> p c j i", i=4)
            if v > 0:
                nc.vector.tensor_copy(out=dst[:, 0 : v // 4], in_=src[:, 0 : v // 4])
            if v < width:
                nc.scalar.copy(out=dst[:, v // 4 : width // 4], in_=src[:, v // 4 : width // 4])
            cols = slice(first, first + width)
            nc.vector.quantize_mx(
                out=u_codes[n][:, cols].bitcast(FP8X4),
                scales=u_scales[n][:, cols],
                in_=u_grp[n][:, cols, :].rearrange("p w j -> p (w j)"),
            )

        def base(a, n):
            for j in range(2):
                js = slice(P * j, P * (j + 1))
                nc.tensor.matmul_mx(
                    out=o_ps[j][n][:],
                    lhsT=v_codes[a][:, js].bitcast(FP8X4),
                    lhsT_scale=v_scales[a][:, js],
                    rhs=w4[:, a, 1024 * n : 1024 * (n + 1)].bitcast(FP4X4),
                    rhs_scale=w4_bytes[:, a * M + N_TILE * n : a * M + N_TILE * (n + 1)],
                    start=(a == 0),
                    stop=False,
                )

        def low_rank(a):
            for t in range(4):
                ts = slice(P * t, P * (t + 1))
                nc.tensor.matmul_mx(
                    out=h_ps[t][:],
                    lhsT=d_codes[a][:, ts].bitcast(FP8X4),
                    lhsT_scale=d_scales[a][:, ts],
                    rhs=v_codes[a][:].bitcast(FP8X4),
                    rhs_scale=v_scales[a][:],
                    start=(a == 0),
                    stop=(a == PASSES - 1),
                )

        def close(c):
            n, first, width = U_STARTS[c] // N_TILE, U_STARTS[c] % N_TILE, U_WIDTHS[c]
            cols = slice(first, first + width)
            for j in range(2):
                nc.tensor.matmul_mx(
                    out=o_ps[j][n][:, cols],
                    lhsT=h_codes[:, P * j : P * (j + 1)].bitcast(FP8X4),
                    lhsT_scale=h_scales[:, P * j : P * (j + 1)],
                    rhs=u_codes[n][:, cols].bitcast(FP8X4),
                    rhs_scale=u_scales[n][:, cols],
                    start=False,
                    stop=(first + width == N_TILE),
                )

        def store(n, first, width):
            cols = slice(first, first + width)
            for j in range(2):
                if j == 0 and n == 1:
                    nc.vector.tensor_copy(out=o_sb[j][n][:, cols], in_=o_ps[j][n][:, cols])
                else:
                    nc.scalar.copy(out=o_sb[j][n][:, cols], in_=o_ps[j][n][:, cols])
                nc.sync.dma_start(
                    out=out[P * j : P * (j + 1), N_TILE * n + first : N_TILE * n + first + width],
                    in_=o_sb[j][n][:, cols],
                )

        group_down(0)
        for a in range(PASSES):
            gather_scales(a)
        group_down(1)
        quantize_down(0)
        gather_words(0)
        low_rank(0)
        quantize_down(1)
        gather_words(1)
        low_rank(1)
        group_down(2)
        quantize_down(2)
        for a in range(2):
            for n in range(2):
                base(a, n)
        gather_words(2)
        low_rank(2)
        base(2, 0)
        base(2, 1)
        for t in range(4):
            if t < 2:
                nc.vector.tensor_copy(out=h_raw[:, t, :], in_=h_ps[t][:])
            else:
                nc.scalar.copy(out=h_raw[:, t, :], in_=h_ps[t][:])
        nc.vector.tensor_copy(
            out=h_grp[:].rearrange("p (c i) t -> p c t i", i=8),
            in_=h_raw[:].rearrange("p t (c i) -> p c t i", i=8),
        )
        nc.vector.quantize_mx(
            out=h_codes[:].bitcast(FP8X4), scales=h_scales[:], in_=h_grp[:].rearrange("p w j -> p (w j)")
        )
        prepare_up(0)
        prepare_up(1)
        close(0)
        close(1)
        prepare_up(2)
        store(0, 0, N_TILE)
        close(2)
        prepare_up(3)
        close(3)
        store(1, 0, N_TILE // 2)
        store(1, N_TILE // 2, N_TILE // 2)
